import numpy as np
import ml_dtypes


def mxq(x, axis, fmt="e4m3"):
    dtype, down = {"e4m3": (ml_dtypes.float8_e4m3fn, 7), "e5m2": (ml_dtypes.float8_e5m2, 14)}[fmt]
    v = np.moveaxis(np.asarray(x, np.float32).astype(ml_dtypes.bfloat16).astype(np.float64), axis, -1)
    blocks = v.reshape(v.shape[:-1] + (-1, 32))
    amax = np.abs(blocks).max(-1, keepdims=True)
    byte = np.maximum(np.where(amax > 0, np.frexp(amax)[1] - 1 + 127, 0) - down, 1)
    scale = np.exp2(byte - 127.0)
    codes = (blocks / scale).astype(np.float32).astype(dtype).astype(np.float64)
    return np.moveaxis((codes * scale).reshape(v.shape), -1, axis)


WIDE = False


def mx_kscale(k):
    if not WIDE:
        return np.ones(k)
    levels = np.array([10, -10, 5, -5, 0])
    if k % 512:
        return np.exp2(np.random.permutation(np.resize(levels, k // 32))).repeat(32)
    a = np.empty((k // 512, 16))
    for p in range(k // 512):
        a[p, :8] = np.random.permutation(np.resize(levels, 8))
        for g in range(8):
            far = levels[np.abs(levels - a[p, g]) >= 10]
            a[p, g + 8] = far[np.random.randint(len(far))]
    return np.exp2(a.ravel()).repeat(32)


def f64(x):
    return np.asarray(x).astype(np.float64)


def striped(idx):
    return np.tile(idx.reshape(-1, 16).T, (8, 1)).astype(np.uint16)


def unstriped(offs):
    return offs[:16].T.reshape(-1).astype(np.int64)


K, T, E, C, N = 512, 1024, 8, 128, 128


def by_expert(wq, xq):
    return np.concatenate([wq[e].T @ xq[:, e * C:(e + 1) * C] for e in range(E)], axis=1)


def setup_inputs():
    n = np.random.standard_normal
    s = mx_kscale(K)[:, None]
    return {
        "xT": (n((K, T)) * s).astype(np.float32),
        "w": (n((E, K, N)) / np.sqrt(K) / s[None]).astype(np.float32),
        "gate": np.tile(np.random.uniform(0.2, 1.0, E * C), (N, 1)).astype(np.float32),
        "offs": striped(np.random.permutation(T)[:E * C]),
    }


def reference(xT, w, gate, offs):
    idx = unstriped(offs)
    xq = mxq(f64(xT)[:, idx], 0, "e4m3")
    y = by_expert(mxq(f64(w), 1, "e4m3"), xq)
    out = np.zeros((N, T))
    out[:, idx] = f64(gate) * y
    return out

@@ -1,0 +1,128 @@
+from contextlib import ExitStack
+
+import concourse.mybir as mybir
+
+F32 = mybir.dt.float32
+BF16 = mybir.dt.bfloat16
+U32 = mybir.dt.uint32
+U16 = mybir.dt.uint16
+U8 = mybir.dt.uint8
+FP8X4 = mybir.dt.float8_e4m3fn_x4
+MULT = mybir.AluOpType.mult
+ADD = mybir.AluOpType.add
+COPY = mybir.ActivationFunctionType.Copy
+
+P = 128
+K, T, E, C, N = 512, 1024, 8, 128, 128
+FLOPS = 2 * K * N * E * C
+
+SIZES = [256, 256, 128, 128, 128, 128]
+CAST_ENGINES = ["v", "v", "v", "v"]
+W_ENGINES = ["v", "v", "v", "v"]
+LOAD_ORDER = ["x0", "o0", "w0", "x1", "w1", "x2", "w2", "x3", "g0", "w3", "g1"]
+HOLD_BACK = False
+STORE_SPLIT = 1
+GATE_PIECES = 2
+
+
+def tile_routed_moe_kernel(tc, xT, w, gate, offs, out):
+    nc = tc.nc
+
+    def copy_on(engine, dst, src):
+        if engine == "v":
+            nc.vector.tensor_copy(dst, src)
+        elif engine == "s":
+            nc.scalar.copy(dst, src)
+        else:
+            nc.gpsimd.tensor_scalar(dst, src, 1.0, 0.0, MULT, ADD)
+
+    with ExitStack() as ctx:
+        lists = ctx.enter_context(tc.tile_pool(name="lists", bufs=1))
+        keep = ctx.enter_context(tc.tile_pool(name="keep", bufs=1))
+        psum = ctx.enter_context(tc.psum_pool(name="psum", bufs=1))
+
+        offs_t = lists.tile([P, E * C // 16], U16, name="offs_t")
+        x_view = xT.rearrange("(p t) n -> p t n", t=4)
+        plane = []
+        for t in range(4):
+            if t == 3 and HOLD_BACK:
+                plane.append(keep.tile([P, T], F32, name="plane3", tag="shared", align_bytes=64))
+            else:
+                plane.append(keep.tile([P, T], F32, name="plane%d" % t))
+        w_raw = [keep.tile([P, 2, 4, N], F32, name="w_raw%d" % i) for i in range(E // 2)]
+        gate_w = E * C // GATE_PIECES
+        gate_t = [keep.tile([P, gate_w], F32, name="gate_t%d" % i) for i in range(GATE_PIECES)]
+        for what in LOAD_ORDER:
+            i = int(what[1])
+            if what[0] == "o":
+                nc.sync.dma_start(offs_t[:], offs)
+            elif what[0] == "x":
+                nc.sync.dma_start(plane[i][:], x_view[:, i, :])
+            elif what[0] == "w":
+                nc.sync.dma_start(w_raw[i][:], w[2 * i:2 * i + 2].rearrange("e (p j) n -> p e j n", j=4))
+            else:
+                nc.sync.dma_start(gate_t[i][:], gate[:, i * gate_w:(i + 1) * gate_w])
+
+        warm_in = keep.tile([P, 1], F32, name="warm_in")
+        warm_out = keep.tile([P, 1], F32, name="warm_out")
+        nc.vector.memset(warm_in[:], 0.0)
+        nc.scalar.activation(warm_out[:], warm_in[:], COPY)
+
+        plane_bf = keep.tile([P, 4, T], BF16, name="plane_bf")
+        for t in range(4):
+            copy_on(CAST_ENGINES[t], plane_bf[:, t, :], plane[t][:])
+
+        ring = ctx.enter_context(tc.tile_pool(name="ring", bufs=2))
+
+        w_codes = []
+        w_scales = []
+
+        def weights(i):
+            w_grp = keep.tile([P, 2, N, 4], BF16, name="w_grp%d" % i, align_bytes=64)
+            copy_on(W_ENGINES[i], w_grp[:], w_raw[i][:].rearrange("p e j n -> p e n j"))
+            w_codes.append(keep.tile([P, 2 * N], U32, name="w_codes%d" % i, align_bytes=64))
+            w_scales.append(keep.tile([P, 2 * N], U8, name="w_scales%d" % i, align_bytes=64))
+            nc.vector.quantize_mx(
+                out=w_codes[i][:].bitcast(FP8X4), scales=w_scales[i][:],
+                in_=w_grp[:].rearrange("p e n j -> p (e n j)"),
+            )
+
+        out_w = keep.tile([P, T], F32, name="out_w")
+
+        first = 0
+        for c in range(len(SIZES)):
+            n = SIZES[c]
+            some = offs_t[:, first // 16:(first + n) // 16]
+            x_tile = ring.tile([P, n, 4], BF16, name="x_grp%d" % c, tag="x_grp", align_bytes=64)
+            x_grp = x_tile[:]
+            for t in range(4):
+                nc.scalar.activation(x_grp[:, :, t], plane_bf[:, t, :].indirect(some), COPY)
+            while len(w_codes) * 2 * C < first + n:
+                weights(len(w_codes))
+            x_codes = keep.tile([P, n], U32, name="x_codes%d" % c, align_bytes=64)
+            x_scales = keep.tile([P, n], U8, name="x_scales%d" % c, align_bytes=64)
+            nc.vector.quantize_mx(
+                out=x_codes[:].bitcast(FP8X4), scales=x_scales[:],
+                in_=x_grp.rearrange("p n t -> p (n t)"),
+            )
+            acc = psum.tile([P, n], F32, name="acc%d" % c)
+            for s in range(n // C):
+                e = first // C + s
+                here = slice(s * C, (s + 1) * C)
+                wcols = slice((e % 2) * N, (e % 2 + 1) * N)
+                nc.tensor.matmul_mx(
+                    out=acc[:, here],
+                    lhsT=w_codes[e // 2][:, wcols].bitcast(FP8X4), lhsT_scale=w_scales[e // 2][:, wcols],
+                    rhs=x_codes[:, here].bitcast(FP8X4), rhs_scale=x_scales[:, here],
+                    start=True, stop=True,
+                )
+            y = keep.tile([P, n], F32, name="y%d" % c)
+            gi = first // gate_w
+            nc.vector.tensor_tensor(y[:], acc[:], gate_t[gi][:, first - gi * gate_w:first - gi * gate_w + n], MULT)
+            nc.vector.tensor_copy(out_w[:].indirect(some), y[:])
+            first += n
+
+        step = T // STORE_SPLIT
+        for s in range(STORE_SPLIT):
+            queue = nc.sync if s % 2 == 0 else nc.scalar
+            queue.dma_start(out[:, s * step:(s + 1) * step], out_w[:, s * step:(s + 1) * step])

@@ -16,13 +16,14 @@ P = 128
 K, T, E, C, N = 512, 1024, 8, 128, 128
 FLOPS = 2 * K * N * E * C
 
-SIZES = [256, 256, 128, 128, 128, 128]
+SIZES = [128] * 8
+OUT_ENGINES = ["v"] * 8
 CAST_ENGINES = ["v", "v", "v", "v"]
-W_ENGINES = ["v", "v", "v", "v"]
-LOAD_ORDER = ["x0", "o0", "w0", "x1", "w1", "x2", "w2", "x3", "g0", "w3", "g1"]
-HOLD_BACK = False
+W_ENGINES = ["g", "g", "g", "g"]
+LOAD_ORDER = ["x0", "o0", "x1", "x2", "w0", "x3", "g0", "w1", "w2", "w3", "g1"]
 STORE_SPLIT = 1
 GATE_PIECES = 2
+SCATTER_LAG = 0
 
 
 def tile_routed_moe_kernel(tc, xT, w, gate, offs, out):
@@ -43,13 +44,8 @@ def tile_routed_moe_kernel(tc, xT, w, gate, offs, out):
 
         offs_t = lists.tile([P, E * C // 16], U16, name="offs_t")
         x_view = xT.rearrange("(p t) n -> p t n", t=4)
-        plane = []
-        for t in range(4):
-            if t == 3 and HOLD_BACK:
-                plane.append(keep.tile([P, T], F32, name="plane3", tag="shared", align_bytes=64))
-            else:
-                plane.append(keep.tile([P, T], F32, name="plane%d" % t))
-        w_raw = [keep.tile([P, 2, 4, N], F32, name="w_raw%d" % i) for i in range(E // 2)]
+        plane = [keep.tile([P, T], F32, name="plane%d" % t) for t in range(4)]
+        w_raw = [keep.tile([P, 2, 4, N], F32, name="w_raw%d" % i, tag="after_raw%d" % i, align_bytes=64) for i in range(E // 2)]
         gate_w = E * C // GATE_PIECES
         gate_t = [keep.tile([P, gate_w], F32, name="gate_t%d" % i) for i in range(GATE_PIECES)]
         for what in LOAD_ORDER:
@@ -72,13 +68,10 @@ def tile_routed_moe_kernel(tc, xT, w, gate, offs, out):
         for t in range(4):
             copy_on(CAST_ENGINES[t], plane_bf[:, t, :], plane[t][:])
 
-        ring = ctx.enter_context(tc.tile_pool(name="ring", bufs=2))
-
         w_codes = []
         w_scales = []
-
-        def weights(i):
-            w_grp = keep.tile([P, 2, N, 4], BF16, name="w_grp%d" % i, align_bytes=64)
+        for i in range(E // 2):
+            w_grp = keep.tile([P, 2, N, 4], BF16, name="w_grp%d" % i, tag="after_grp%d" % i, align_bytes=64)
             copy_on(W_ENGINES[i], w_grp[:], w_raw[i][:].rearrange("p e j n -> p e n j"))
             w_codes.append(keep.tile([P, 2 * N], U32, name="w_codes%d" % i, align_bytes=64))
             w_scales.append(keep.tile([P, 2 * N], U8, name="w_scales%d" % i, align_bytes=64))
@@ -87,27 +80,38 @@ def tile_routed_moe_kernel(tc, xT, w, gate, offs, out):
                 in_=w_grp[:].rearrange("p e n j -> p (e n j)"),
             )
 
+        ring = ctx.enter_context(tc.tile_pool(name="ring", bufs=3))
         out_w = keep.tile([P, T], F32, name="out_w")
+        starts = [sum(SIZES[:c]) for c in range(len(SIZES))]
+        y = [keep.tile([P, SIZES[c]], F32, name="y%d" % c) for c in range(len(SIZES))]
 
-        first = 0
+        def some(c):
+            return offs_t[:, starts[c] // 16:(starts[c] + SIZES[c]) // 16]
+
+        def gate_of(c):
+            gi = starts[c] // gate_w
+            return gate_t[gi][:, starts[c] - gi * gate_w:starts[c] - gi * gate_w + SIZES[c]]
+
+        def scatter(c):
+            if OUT_ENGINES[c] == "v":
+                nc.vector.tensor_copy(out_w[:].indirect(some(c)), y[c][:])
+            else:
+                nc.vector.tensor_tensor(out_w[:].indirect(some(c)), y[c][:], gate_of(c), MULT)
+
         for c in range(len(SIZES)):
             n = SIZES[c]
-            some = offs_t[:, first // 16:(first + n) // 16]
-            x_tile = ring.tile([P, n, 4], BF16, name="x_grp%d" % c, tag="x_grp", align_bytes=64)
-            x_grp = x_tile[:]
+            x_grp = ring.tile([P, n, 4], BF16, name="x_grp%d" % c, tag="x_grp", align_bytes=64)
             for t in range(4):
-                nc.scalar.activation(x_grp[:, :, t], plane_bf[:, t, :].indirect(some), COPY)
-            while len(w_codes) * 2 * C < first + n:
-                weights(len(w_codes))
-            x_codes = keep.tile([P, n], U32, name="x_codes%d" % c, align_bytes=64)
+                nc.scalar.activation(x_grp[:, :, t], plane_bf[:, t, :].indirect(some(c)), COPY)
+            x_codes = keep.tile([P, n], U32, name="x_codes%d" % c, tag=("after_grp%d" if c % 2 == 0 else "after_raw%d") % (c // 2), align_bytes=64)
             x_scales = keep.tile([P, n], U8, name="x_scales%d" % c, align_bytes=64)
             nc.vector.quantize_mx(
                 out=x_codes[:].bitcast(FP8X4), scales=x_scales[:],
-                in_=x_grp.rearrange("p n t -> p (n t)"),
+                in_=x_grp[:].rearrange("p n t -> p (n t)"),
             )
             acc = psum.tile([P, n], F32, name="acc%d" % c)
             for s in range(n // C):
-                e = first // C + s
+                e = starts[c] // C + s
                 here = slice(s * C, (s + 1) * C)
                 wcols = slice((e % 2) * N, (e % 2 + 1) * N)
                 nc.tensor.matmul_mx(
@@ -116,11 +120,14 @@ def tile_routed_moe_kernel(tc, xT, w, gate, offs, out):
                     rhs=x_codes[:, here].bitcast(FP8X4), rhs_scale=x_scales[:, here],
                     start=True, stop=True,
                 )
-            y = keep.tile([P, n], F32, name="y%d" % c)
-            gi = first // gate_w
-            nc.vector.tensor_tensor(y[:], acc[:], gate_t[gi][:, first - gi * gate_w:first - gi * gate_w + n], MULT)
-            nc.vector.tensor_copy(out_w[:].indirect(some), y[:])
-            first += n
+            if OUT_ENGINES[c] == "v":
+                nc.vector.tensor_tensor(y[c][:], acc[:], gate_of(c), MULT)
+            else:
+                nc.scalar.copy(y[c][:], acc[:])
+            if c >= SCATTER_LAG:
+                scatter(c - SCATTER_LAG)
+        for c in range(max(0, len(SIZES) - SCATTER_LAG), len(SIZES)):
+            scatter(c)
 
         step = T // STORE_SPLIT
         for s in range(STORE_SPLIT):

@@ -16,11 +16,11 @@ P = 128
 K, T, E, C, N = 512, 1024, 8, 128, 128
 FLOPS = 2 * K * N * E * C
 
-SIZES = [128] * 8
-OUT_ENGINES = ["v"] * 8
+SIZES = [256, 128, 128, 128, 128, 128, 128]
+OUT_ENGINES = ["s"] * 7
 CAST_ENGINES = ["v", "v", "v", "v"]
-W_ENGINES = ["g", "g", "g", "g"]
-LOAD_ORDER = ["x0", "o0", "x1", "x2", "w0", "x3", "g0", "w1", "w2", "w3", "g1"]
+W_ENGINES = ["v", "v", "v", "v"]
+LOAD_ORDER = ["x0", "o0", "x1", "w0", "x2", "w1", "x3", "g0", "w2", "w3", "g1"]
 STORE_SPLIT = 1
 GATE_PIECES = 2
 SCATTER_LAG = 0
@@ -45,7 +45,7 @@ def tile_routed_moe_kernel(tc, xT, w, gate, offs, out):
         offs_t = lists.tile([P, E * C // 16], U16, name="offs_t")
         x_view = xT.rearrange("(p t) n -> p t n", t=4)
         plane = [keep.tile([P, T], F32, name="plane%d" % t) for t in range(4)]
-        w_raw = [keep.tile([P, 2, 4, N], F32, name="w_raw%d" % i, tag="after_raw%d" % i, align_bytes=64) for i in range(E // 2)]
+        w_raw = [keep.tile([P, 2, 4, N], F32, name="w_raw%d" % i) for i in range(E // 2)]
         gate_w = E * C // GATE_PIECES
         gate_t = [keep.tile([P, gate_w], F32, name="gate_t%d" % i) for i in range(GATE_PIECES)]
         for what in LOAD_ORDER:
@@ -71,7 +71,7 @@ def tile_routed_moe_kernel(tc, xT, w, gate, offs, out):
         w_codes = []
         w_scales = []
         for i in range(E // 2):
-            w_grp = keep.tile([P, 2, N, 4], BF16, name="w_grp%d" % i, tag="after_grp%d" % i, align_bytes=64)
+            w_grp = keep.tile([P, 2, N, 4], BF16, name="w_grp%d" % i, align_bytes=64)
             copy_on(W_ENGINES[i], w_grp[:], w_raw[i][:].rearrange("p e j n -> p e n j"))
             w_codes.append(keep.tile([P, 2 * N], U32, name="w_codes%d" % i, align_bytes=64))
             w_scales.append(keep.tile([P, 2 * N], U8, name="w_scales%d" % i, align_bytes=64))
@@ -103,7 +103,7 @@ def tile_routed_moe_kernel(tc, xT, w, gate, offs, out):
             x_grp = ring.tile([P, n, 4], BF16, name="x_grp%d" % c, tag="x_grp", align_bytes=64)
             for t in range(4):
                 nc.scalar.activation(x_grp[:, :, t], plane_bf[:, t, :].indirect(some(c)), COPY)
-            x_codes = keep.tile([P, n], U32, name="x_codes%d" % c, tag=("after_grp%d" if c % 2 == 0 else "after_raw%d") % (c // 2), align_bytes=64)
+            x_codes = keep.tile([P, n], U32, name="x_codes%d" % c, align_bytes=64)
             x_scales = keep.tile([P, n], U8, name="x_scales%d" % c, align_bytes=64)
             nc.vector.quantize_mx(
                 out=x_codes[:].bitcast(FP8X4), scales=x_scales[:],
@@ -123,7 +123,7 @@ def tile_routed_moe_kernel(tc, xT, w, gate, offs, out):
             if OUT_ENGINES[c] == "v":
                 nc.vector.tensor_tensor(y[c][:], acc[:], gate_of(c), MULT)
             else:
-                nc.scalar.copy(y[c][:], acc[:])
+                nc.scalar.activation(y[c][:], acc[:], COPY)
             if c >= SCATTER_LAG:
                 scatter(c - SCATTER_LAG)
         for c in range(max(0, len(SIZES) - SCATTER_LAG), len(SIZES)):

@@ -16,7 +16,9 @@ P = 128
 K, T, E, C, N = 512, 1024, 8, 128, 128
 FLOPS = 2 * K * N * E * C
 
-SIZES = [256, 128, 128, 128, 128, 128, 128]
+SIZES = [128, 128, 256, 128, 128, 128, 128]
+ROADS = ["a", "f", "f", "f", "f", "f", "f"]
+MIX_ENGINE = "v"
 OUT_ENGINES = ["s"] * 7
 CAST_ENGINES = ["v", "v", "v", "v"]
 W_ENGINES = ["v", "v", "v", "v"]
@@ -100,9 +102,16 @@ def tile_routed_moe_kernel(tc, xT, w, gate, offs, out):
 
         for c in range(len(SIZES)):
             n = SIZES[c]
-            x_grp = ring.tile([P, n, 4], BF16, name="x_grp%d" % c, tag="x_grp", align_bytes=64)
-            for t in range(4):
-                nc.scalar.activation(x_grp[:, :, t], plane_bf[:, t, :].indirect(some(c)), COPY)
+            if ROADS[c] == "a":
+                x_grp = keep.tile([P, n, 4], BF16, name="x_grp%d" % c, align_bytes=64)
+                g4 = keep.tile([P, 4, n], F32, name="g4_%d" % c)
+                for t in range(4):
+                    nc.vector.tensor_copy(g4[:, t, :], plane[t][:].indirect(some(c)))
+                copy_on(MIX_ENGINE, x_grp[:], g4[:].rearrange("p t n -> p n t"))
+            else:
+                x_grp = ring.tile([P, n, 4], BF16, name="x_grp%d" % c, tag="x_grp", align_bytes=64)
+                for t in range(4):
+                    nc.scalar.activation(x_grp[:, :, t], plane_bf[:, t, :].indirect(some(c)), COPY)
             x_codes = keep.tile([P, n], U32, name="x_codes%d" % c, align_bytes=64)
             x_scales = keep.tile([P, n], U8, name="x_scales%d" % c, align_bytes=64)
             nc.vector.quantize_mx(

@@ -74,7 +74,11 @@ def tile_routed_moe_kernel(tc, xT, w, gate, offs, out):
         w_scales = []
         for i in range(E // 2):
             w_grp = keep.tile([P, 2, N, 4], BF16, name="w_grp%d" % i, align_bytes=64)
-            copy_on(W_ENGINES[i], w_grp[:], w_raw[i][:].rearrange("p e j n -> p e n j"))
+            copy_on(
+                W_ENGINES[i],
+                w_grp[:].rearrange("p e (c i) j -> p e c j i", i=4),
+                w_raw[i][:].rearrange("p e j (c i) -> p e c j i", i=4),
+            )
             w_codes.append(keep.tile([P, 2 * N], U32, name="w_codes%d" % i, align_bytes=64))
             w_scales.append(keep.tile([P, 2 * N], U8, name="w_scales%d" % i, align_bytes=64))
             nc.vector.quantize_mx(
@@ -107,7 +111,11 @@ def tile_routed_moe_kernel(tc, xT, w, gate, offs, out):
                 g4 = keep.tile([P, 4, n], F32, name="g4_%d" % c)
                 for t in range(4):
                     nc.vector.tensor_copy(g4[:, t, :], plane[t][:].indirect(some(c)))
-                copy_on(MIX_ENGINE, x_grp[:], g4[:].rearrange("p t n -> p n t"))
+                copy_on(
+                    MIX_ENGINE,
+                    x_grp[:].rearrange("p (c i) t -> p c t i", i=4),
+                    g4[:].rearrange("p t (c i) -> p c t i", i=4),
+                )
             else:
                 x_grp = ring.tile([P, n, 4], BF16, name="x_grp%d" % c, tag="x_grp", align_bytes=64)
                 for t in range(4):

@@ -16,16 +16,19 @@ P = 128
 K, T, E, C, N = 512, 1024, 8, 128, 128
 FLOPS = 2 * K * N * E * C
 
-SIZES = [128, 128, 256, 128, 128, 128, 128]
-ROADS = ["a", "f", "f", "f", "f", "f", "f"]
+SIZES = [256,128,128,128,128,128,128]
+ROADS = ["b","f","f","f","f","f","f"]
 MIX_ENGINE = "v"
-OUT_ENGINES = ["s"] * 7
-CAST_ENGINES = ["v", "v", "v", "v"]
-W_ENGINES = ["v", "v", "v", "v"]
-LOAD_ORDER = ["x0", "o0", "x1", "w0", "x2", "w1", "x3", "g0", "w2", "w3", "g1"]
-STORE_SPLIT = 1
+OUT_ENGINES = ["s","s","s","s","s","s","s"]
+CAST_ENGINES = ["s","s","v","v"]
+W_ENGINES = ["v","v","v","v"]
+LOAD_ORDER = ["x0","o0","x1","w0","x2","w1","x3","g0","w2","w3","g1"]
+RING = 3
+FAST = True
 GATE_PIECES = 2
-SCATTER_LAG = 0
+XSPLIT = [1,1,1,1]
+SPIN = 0
+PINS = {}
 
 
 def tile_routed_moe_kernel(tc, xT, w, gate, offs, out):
@@ -35,7 +38,7 @@ def tile_routed_moe_kernel(tc, xT, w, gate, offs, out):
         if engine == "v":
             nc.vector.tensor_copy(dst, src)
         elif engine == "s":
-            nc.scalar.copy(dst, src)
+            nc.scalar.activation(dst, src, COPY)
         else:
             nc.gpsimd.tensor_scalar(dst, src, 1.0, 0.0, MULT, ADD)
 
@@ -55,7 +58,9 @@ def tile_routed_moe_kernel(tc, xT, w, gate, offs, out):
             if what[0] == "o":
                 nc.sync.dma_start(offs_t[:], offs)
             elif what[0] == "x":
-                nc.sync.dma_start(plane[i][:], x_view[:, i, :])
+                for h in range(XSPLIT[i]):
+                    cols = slice(h * T // XSPLIT[i], (h + 1) * T // XSPLIT[i])
+                    nc.sync.dma_start(plane[i][:, cols], x_view[:, i, cols])
             elif what[0] == "w":
                 nc.sync.dma_start(w_raw[i][:], w[2 * i:2 * i + 2].rearrange("e (p j) n -> p e j n", j=4))
             else:
@@ -68,17 +73,22 @@ def tile_routed_moe_kernel(tc, xT, w, gate, offs, out):
 
         plane_bf = keep.tile([P, 4, T], BF16, name="plane_bf")
         for t in range(4):
-            copy_on(CAST_ENGINES[t], plane_bf[:, t, :], plane[t][:])
+            for h in range(XSPLIT[t]):
+                cols = slice(h * T // XSPLIT[t], (h + 1) * T // XSPLIT[t])
+                copy_on(CAST_ENGINES[t], plane_bf[:, t, cols], plane[t][:, cols])
 
         w_codes = []
         w_scales = []
         for i in range(E // 2):
-            w_grp = keep.tile([P, 2, N, 4], BF16, name="w_grp%d" % i, align_bytes=64)
-            copy_on(
-                W_ENGINES[i],
-                w_grp[:].rearrange("p e (c i) j -> p e c j i", i=4),
-                w_raw[i][:].rearrange("p e j (c i) -> p e c j i", i=4),
-            )
+            w_grp = keep.tile([P, 2, N, 4], BF16, name="w_grp%d" % i, tag="pin%d" % i, align_bytes=64)
+            if FAST:
+                copy_on(
+                    W_ENGINES[i],
+                    w_grp[:].rearrange("p e (c i) j -> p e c j i", i=4),
+                    w_raw[i][:].rearrange("p e j (c i) -> p e c j i", i=4),
+                )
+            else:
+                copy_on(W_ENGINES[i], w_grp[:], w_raw[i][:].rearrange("p e j n -> p e n j"))
             w_codes.append(keep.tile([P, 2 * N], U32, name="w_codes%d" % i, align_bytes=64))
             w_scales.append(keep.tile([P, 2 * N], U8, name="w_scales%d" % i, align_bytes=64))
             nc.vector.quantize_mx(
@@ -86,10 +96,10 @@ def tile_routed_moe_kernel(tc, xT, w, gate, offs, out):
                 in_=w_grp[:].rearrange("p e n j -> p (e n j)"),
             )
 
-        ring = ctx.enter_context(tc.tile_pool(name="ring", bufs=3))
+        ring = ctx.enter_context(tc.tile_pool(name="ring", bufs=RING))
         out_w = keep.tile([P, T], F32, name="out_w")
         starts = [sum(SIZES[:c]) for c in range(len(SIZES))]
-        y = [keep.tile([P, SIZES[c]], F32, name="y%d" % c) for c in range(len(SIZES))]
+        y = []
 
         def some(c):
             return offs_t[:, starts[c] // 16:(starts[c] + SIZES[c]) // 16]
@@ -111,16 +121,43 @@ def tile_routed_moe_kernel(tc, xT, w, gate, offs, out):
                 g4 = keep.tile([P, 4, n], F32, name="g4_%d" % c)
                 for t in range(4):
                     nc.vector.tensor_copy(g4[:, t, :], plane[t][:].indirect(some(c)))
-                copy_on(
-                    MIX_ENGINE,
-                    x_grp[:].rearrange("p (c i) t -> p c t i", i=4),
-                    g4[:].rearrange("p t (c i) -> p c t i", i=4),
-                )
-            else:
+                if FAST:
+                    copy_on(
+                        MIX_ENGINE,
+                        x_grp[:].rearrange("p (c i) t -> p c t i", i=4),
+                        g4[:].rearrange("p t (c i) -> p c t i", i=4),
+                    )
+                else:
+                    copy_on(MIX_ENGINE, x_grp[:], g4[:].rearrange("p t n -> p n t"))
+            elif ROADS[c] == "h":
+                x_grp = keep.tile([P, n, 4], BF16, name="x_grp%d" % c, align_bytes=64)
+                for t in range(2):
+                    nc.vector.tensor_copy(x_grp[:, :, t], plane[t][:].indirect(some(c)))
+                for t in range(2, 4):
+                    nc.scalar.activation(x_grp[:, :, t], plane_bf[:, t, :].indirect(some(c)), COPY)
+            elif ROADS[c] == "b":
+                x_grp = keep.tile([P, n, 4], BF16, name="x_grp%d" % c, align_bytes=64)
+                for t in range(4):
+                    nc.vector.tensor_copy(x_grp[:, :, t], plane[t][:].indirect(some(c)))
+            elif ROADS[c] == "f":
                 x_grp = ring.tile([P, n, 4], BF16, name="x_grp%d" % c, tag="x_grp", align_bytes=64)
                 for t in range(4):
                     nc.scalar.activation(x_grp[:, :, t], plane_bf[:, t, :].indirect(some(c)), COPY)
-            x_codes = keep.tile([P, n], U32, name="x_codes%d" % c, align_bytes=64)
+            else:
+                x_pair = ring.tile([P, 2, n, 2], BF16, name="x_pair%d" % c, tag="x_pair", align_bytes=64)
+                for t in range(4):
+                    nc.scalar.activation(x_pair[:, t // 2, :, t % 2], plane_bf[:, t, :].indirect(some(c)), COPY)
+                x_grp = keep.tile([P, n, 4], BF16, name="x_grp%d" % c, align_bytes=64)
+                nc.vector.tensor_copy(
+                    x_grp[:].rearrange("p n t -> p (n t)").bitcast(F32).rearrange("p (n u) -> p n u", u=2),
+                    x_pair[:].rearrange("p u n e -> p (u n e)").bitcast(F32).rearrange("p (u n) -> p n u", u=2),
+                )
+            if c in PINS:
+                x_codes = keep.tile([P, n], U32, name="x_codes%d" % c, tag="pin%d" % PINS[c], align_bytes=64)
+            elif SPIN and c >= 0:
+                x_codes = keep.tile([P, n], U32, name="x_codes%d" % c, tag="y%d" % (c - SPIN), align_bytes=64)
+            else:
+                x_codes = keep.tile([P, n], U32, name="x_codes%d" % c, align_bytes=64)
             x_scales = keep.tile([P, n], U8, name="x_scales%d" % c, align_bytes=64)
             nc.vector.quantize_mx(
                 out=x_codes[:].bitcast(FP8X4), scales=x_scales[:],
@@ -137,16 +174,11 @@ def tile_routed_moe_kernel(tc, xT, w, gate, offs, out):
                     rhs=x_codes[:, here].bitcast(FP8X4), rhs_scale=x_scales[:, here],
                     start=True, stop=True,
                 )
+            y.append(keep.tile([P, n], F32, name="y%d" % c, tag="y%d" % c, align_bytes=64))
             if OUT_ENGINES[c] == "v":
                 nc.vector.tensor_tensor(y[c][:], acc[:], gate_of(c), MULT)
             else:
                 nc.scalar.activation(y[c][:], acc[:], COPY)
-            if c >= SCATTER_LAG:
-                scatter(c - SCATTER_LAG)
-        for c in range(max(0, len(SIZES) - SCATTER_LAG), len(SIZES)):
             scatter(c)
 
-        step = T // STORE_SPLIT
-        for s in range(STORE_SPLIT):
-            queue = nc.sync if s % 2 == 0 else nc.scalar
-            queue.dma_start(out[:, s * step:(s + 1) * step], out_w[:, s * step:(s + 1) * step])
+        nc.sync.dma_start(out[:, 0:T], out_w[:, 0:T])

@@ -22,7 +22,7 @@ MIX_ENGINE = "v"
 OUT_ENGINES = ["s","s","s","s","s","s","s"]
 CAST_ENGINES = ["s","s","v","v"]
 W_ENGINES = ["v","v","v","v"]
-LOAD_ORDER = ["x0","o0","x1","w0","x2","w1","x3","g0","w2","w3","g1"]
+LOAD_ORDER = ["x0","o0","x1","w0","x2","w1","x3","w2","g0","w3","g1"]
 RING = 3
 FAST = True
 GATE_PIECES = 2

@@ -25,9 +25,10 @@ W_ENGINES = ["v","v","v","v"]
 LOAD_ORDER = ["x0","o0","x1","w0","x2","w1","x3","w2","g0","w3","g1"]
 RING = 3
 FAST = True
-GATE_PIECES = 2
-XSPLIT = [1,1,1,1]
-SPIN = 0
+GATE_CUTS = [0,512,1024]
+XSPLIT = [2,1,1,2]
+SPINS = {}
+SCATTER_AFTER = [[0],[1],[2],[3],[4],[5],[6]]
 PINS = {}
 
 
@@ -51,8 +52,7 @@ def tile_routed_moe_kernel(tc, xT, w, gate, offs, out):
         x_view = xT.rearrange("(p t) n -> p t n", t=4)
         plane = [keep.tile([P, T], F32, name="plane%d" % t) for t in range(4)]
         w_raw = [keep.tile([P, 2, 4, N], F32, name="w_raw%d" % i) for i in range(E // 2)]
-        gate_w = E * C // GATE_PIECES
-        gate_t = [keep.tile([P, gate_w], F32, name="gate_t%d" % i) for i in range(GATE_PIECES)]
+        gate_t = [keep.tile([P, GATE_CUTS[i + 1] - GATE_CUTS[i]], F32, name="gate_t%d" % i) for i in range(len(GATE_CUTS) - 1)]
         for what in LOAD_ORDER:
             i = int(what[1])
             if what[0] == "o":
@@ -64,7 +64,7 @@ def tile_routed_moe_kernel(tc, xT, w, gate, offs, out):
             elif what[0] == "w":
                 nc.sync.dma_start(w_raw[i][:], w[2 * i:2 * i + 2].rearrange("e (p j) n -> p e j n", j=4))
             else:
-                nc.sync.dma_start(gate_t[i][:], gate[:, i * gate_w:(i + 1) * gate_w])
+                nc.sync.dma_start(gate_t[i][:], gate[:, GATE_CUTS[i]:GATE_CUTS[i + 1]])
 
         warm_in = keep.tile([P, 1], F32, name="warm_in")
         warm_out = keep.tile([P, 1], F32, name="warm_out")
@@ -81,7 +81,7 @@ def tile_routed_moe_kernel(tc, xT, w, gate, offs, out):
         w_scales = []
         for i in range(E // 2):
             w_grp = keep.tile([P, 2, N, 4], BF16, name="w_grp%d" % i, tag="pin%d" % i, align_bytes=64)
-            if FAST:
+            if FAST and W_ENGINES[i] == "v":
                 copy_on(
                     W_ENGINES[i],
                     w_grp[:].rearrange("p e (c i) j -> p e c j i", i=4),
@@ -105,8 +105,8 @@ def tile_routed_moe_kernel(tc, xT, w, gate, offs, out):
             return offs_t[:, starts[c] // 16:(starts[c] + SIZES[c]) // 16]
 
         def gate_of(c):
-            gi = starts[c] // gate_w
-            return gate_t[gi][:, starts[c] - gi * gate_w:starts[c] - gi * gate_w + SIZES[c]]
+            gi = max(i for i in range(len(GATE_CUTS) - 1) if GATE_CUTS[i] <= starts[c])
+            return gate_t[gi][:, starts[c] - GATE_CUTS[gi]:starts[c] - GATE_CUTS[gi] + SIZES[c]]
 
         def scatter(c):
             if OUT_ENGINES[c] == "v":
@@ -154,8 +154,8 @@ def tile_routed_moe_kernel(tc, xT, w, gate, offs, out):
                 )
             if c in PINS:
                 x_codes = keep.tile([P, n], U32, name="x_codes%d" % c, tag="pin%d" % PINS[c], align_bytes=64)
-            elif SPIN and c >= 0:
-                x_codes = keep.tile([P, n], U32, name="x_codes%d" % c, tag="y%d" % (c - SPIN), align_bytes=64)
+            elif c in SPINS:
+                x_codes = keep.tile([P, n], U32, name="x_codes%d" % c, tag="y%d" % SPINS[c], align_bytes=64)
             else:
                 x_codes = keep.tile([P, n], U32, name="x_codes%d" % c, align_bytes=64)
             x_scales = keep.tile([P, n], U8, name="x_scales%d" % c, align_bytes=64)
@@ -179,6 +179,7 @@ def tile_routed_moe_kernel(tc, xT, w, gate, offs, out):
                 nc.vector.tensor_tensor(y[c][:], acc[:], gate_of(c), MULT)
             else:
                 nc.scalar.activation(y[c][:], acc[:], COPY)
-            scatter(c)
+            for d in SCATTER_AFTER[c]:
+                scatter(d)
 
         nc.sync.dma_start(out[:, 0:T], out_w[:, 0:T])

@@ -20,8 +20,8 @@ SIZES = [256,128,128,128,128,128,128]
 ROADS = ["b","f","f","f","f","f","f"]
 MIX_ENGINE = "v"
 OUT_ENGINES = ["s","s","s","s","s","s","s"]
-CAST_ENGINES = ["s","s","v","v"]
-W_ENGINES = ["v","v","v","v"]
+CAST_ENGINES = ["s","v","v","v"]
+W_ENGINES = ["v","v","v","s"]
 LOAD_ORDER = ["x0","o0","x1","w0","x2","w1","x3","w2","g0","w3","g1"]
 RING = 3
 FAST = True

@@ -16,10 +16,10 @@ P = 128
 K, T, E, C, N = 512, 1024, 8, 128, 128
 FLOPS = 2 * K * N * E * C
 
-SIZES = [256,128,128,128,128,128,128]
-ROADS = ["b","f","f","f","f","f","f"]
+SIZES = [256,256,128,128,128,128]
+ROADS = ["b","f","f","f","f","f"]
 MIX_ENGINE = "v"
-OUT_ENGINES = ["s","s","s","s","s","s","s"]
+OUT_ENGINES = ["s","s","s","s","s","s"]
 CAST_ENGINES = ["s","v","v","v"]
 W_ENGINES = ["v","v","v","s"]
 LOAD_ORDER = ["x0","o0","x1","w0","x2","w1","x3","w2","g0","w3","g1"]
@@ -28,7 +28,7 @@ FAST = True
 GATE_CUTS = [0,512,1024]
 XSPLIT = [2,1,1,2]
 SPINS = {}
-SCATTER_AFTER = [[0],[1],[2],[3],[4],[5],[6]]
+SCATTER_AFTER = [[0],[1],[2],[3],[4],[5]]
 PINS = {}
 
 

@@ -39,7 +39,7 @@ def tile_routed_moe_kernel(tc, xT, w, gate, offs, out):
         if engine == "v":
             nc.vector.tensor_copy(dst, src)
         elif engine == "s":
-            nc.scalar.activation(dst, src, COPY)
+            nc.scalar.copy(dst, src)
         else:
             nc.gpsimd.tensor_scalar(dst, src, 1.0, 0.0, MULT, ADD)
 
@@ -81,7 +81,7 @@ def tile_routed_moe_kernel(tc, xT, w, gate, offs, out):
         w_scales = []
         for i in range(E // 2):
             w_grp = keep.tile([P, 2, N, 4], BF16, name="w_grp%d" % i, tag="pin%d" % i, align_bytes=64)
-            if FAST and W_ENGINES[i] == "v":
+            if FAST:
                 copy_on(
                     W_ENGINES[i],
                     w_grp[:].rearrange("p e (c i) j -> p e c j i", i=4),
@@ -178,7 +178,7 @@ def tile_routed_moe_kernel(tc, xT, w, gate, offs, out):
             if OUT_ENGINES[c] == "v":
                 nc.vector.tensor_tensor(y[c][:], acc[:], gate_of(c), MULT)
             else:
-                nc.scalar.activation(y[c][:], acc[:], COPY)
+                nc.scalar.copy(y[c][:], acc[:])
             for d in SCATTER_AFTER[c]:
                 scatter(d)
 

@@ -19,7 +19,7 @@ FLOPS = 2 * K * N * E * C
 SIZES = [256,256,128,128,128,128]
 ROADS = ["b","f","f","f","f","f"]
 MIX_ENGINE = "v"
-OUT_ENGINES = ["s","s","s","s","s","s"]
+OUT_ENGINES = ["s","s","s","s","s","v"]
 CAST_ENGINES = ["s","v","v","v"]
 W_ENGINES = ["v","v","v","s"]
 LOAD_ORDER = ["x0","o0","x1","w0","x2","w1","x3","w2","g0","w3","g1"]

@@ -19,7 +19,7 @@ FLOPS = 2 * K * N * E * C
 SIZES = [256,256,128,128,128,128]
 ROADS = ["b","f","f","f","f","f"]
 MIX_ENGINE = "v"
-OUT_ENGINES = ["s","s","s","s","s","v"]
+OUT_ENGINES = ["s","s","s","s","v","v"]
 CAST_ENGINES = ["s","v","v","v"]
 W_ENGINES = ["v","v","v","s"]
 LOAD_ORDER = ["x0","o0","x1","w0","x2","w1","x3","w2","g0","w3","g1"]

@@ -16,20 +16,18 @@ P = 128
 K, T, E, C, N = 512, 1024, 8, 128, 128
 FLOPS = 2 * K * N * E * C
 
-SIZES = [256,256,128,128,128,128]
-ROADS = ["b","f","f","f","f","f"]
-MIX_ENGINE = "v"
-OUT_ENGINES = ["s","s","s","s","v","v"]
+SPINS = {}
+SIZES = [256,256,128,128,256]
+ROADS = ["b","f","f","f","f"]
+OUT_ENGINES = ["s","s","s","s","v"]
 CAST_ENGINES = ["s","v","v","v"]
 W_ENGINES = ["v","v","v","s"]
+WPT = 2
 LOAD_ORDER = ["x0","o0","x1","w0","x2","w1","x3","w2","g0","w3","g1"]
 RING = 3
-FAST = True
 GATE_CUTS = [0,512,1024]
 XSPLIT = [2,1,1,2]
-SPINS = {}
-SCATTER_AFTER = [[0],[1],[2],[3],[4],[5]]
-PINS = {}
+TEXT = ["c0","c1","c2","c3","W0","Q0","W1","Q1","W2","Q2","W3","Q3","G0","q0","m0","o0","s0","G1","q1","m1","o1","s1","G2","q2","m2","o2","s2","G3","q3","m3","o3","s3","G4","q4","m4","o4","s4"]
 
 
 def tile_routed_moe_kernel(tc, xT, w, gate, offs, out):
@@ -47,11 +45,12 @@ def tile_routed_moe_kernel(tc, xT, w, gate, offs, out):
         lists = ctx.enter_context(tc.tile_pool(name="lists", bufs=1))
         keep = ctx.enter_context(tc.tile_pool(name="keep", bufs=1))
         psum = ctx.enter_context(tc.psum_pool(name="psum", bufs=1))
+        ring = ctx.enter_context(tc.tile_pool(name="ring", bufs=max(RING, 1)))
 
         offs_t = lists.tile([P, E * C // 16], U16, name="offs_t")
         x_view = xT.rearrange("(p t) n -> p t n", t=4)
         plane = [keep.tile([P, T], F32, name="plane%d" % t) for t in range(4)]
-        w_raw = [keep.tile([P, 2, 4, N], F32, name="w_raw%d" % i) for i in range(E // 2)]
+        w_raw = [keep.tile([P, WPT, 4, N], F32, name="w_raw%d" % i) for i in range(E // WPT)]
         gate_t = [keep.tile([P, GATE_CUTS[i + 1] - GATE_CUTS[i]], F32, name="gate_t%d" % i) for i in range(len(GATE_CUTS) - 1)]
         for what in LOAD_ORDER:
             i = int(what[1])
@@ -62,7 +61,7 @@ def tile_routed_moe_kernel(tc, xT, w, gate, offs, out):
                     cols = slice(h * T // XSPLIT[i], (h + 1) * T // XSPLIT[i])
                     nc.sync.dma_start(plane[i][:, cols], x_view[:, i, cols])
             elif what[0] == "w":
-                nc.sync.dma_start(w_raw[i][:], w[2 * i:2 * i + 2].rearrange("e (p j) n -> p e j n", j=4))
+                nc.sync.dma_start(w_raw[i][:], w[WPT * i:WPT * i + WPT].rearrange("e (p j) n -> p e j n", j=4))
             else:
                 nc.sync.dma_start(gate_t[i][:], gate[:, GATE_CUTS[i]:GATE_CUTS[i + 1]])
 
@@ -72,34 +71,16 @@ def tile_routed_moe_kernel(tc, xT, w, gate, offs, out):
         nc.scalar.activation(warm_out[:], warm_in[:], COPY)
 
         plane_bf = keep.tile([P, 4, T], BF16, name="plane_bf")
-        for t in range(4):
-            for h in range(XSPLIT[t]):
-                cols = slice(h * T // XSPLIT[t], (h + 1) * T // XSPLIT[t])
-                copy_on(CAST_ENGINES[t], plane_bf[:, t, cols], plane[t][:, cols])
-
-        w_codes = []
-        w_scales = []
-        for i in range(E // 2):
-            w_grp = keep.tile([P, 2, N, 4], BF16, name="w_grp%d" % i, tag="pin%d" % i, align_bytes=64)
-            if FAST:
-                copy_on(
-                    W_ENGINES[i],
-                    w_grp[:].rearrange("p e (c i) j -> p e c j i", i=4),
-                    w_raw[i][:].rearrange("p e j (c i) -> p e c j i", i=4),
-                )
-            else:
-                copy_on(W_ENGINES[i], w_grp[:], w_raw[i][:].rearrange("p e j n -> p e n j"))
-            w_codes.append(keep.tile([P, 2 * N], U32, name="w_codes%d" % i, align_bytes=64))
-            w_scales.append(keep.tile([P, 2 * N], U8, name="w_scales%d" % i, align_bytes=64))
-            nc.vector.quantize_mx(
-                out=w_codes[i][:].bitcast(FP8X4), scales=w_scales[i][:],
-                in_=w_grp[:].rearrange("p e n j -> p (e n j)"),
-            )
-
-        ring = ctx.enter_context(tc.tile_pool(name="ring", bufs=RING))
         out_w = keep.tile([P, T], F32, name="out_w")
         starts = [sum(SIZES[:c]) for c in range(len(SIZES))]
-        y = []
+        w_grp = {}
+        w_codes = {}
+        w_scales = {}
+        x_grp = {}
+        x_codes = {}
+        x_scales = {}
+        acc = {}
+        y = {}
 
         def some(c):
             return offs_t[:, starts[c] // 16:(starts[c] + SIZES[c]) // 16]
@@ -108,78 +89,103 @@ def tile_routed_moe_kernel(tc, xT, w, gate, offs, out):
             gi = max(i for i in range(len(GATE_CUTS) - 1) if GATE_CUTS[i] <= starts[c])
             return gate_t[gi][:, starts[c] - GATE_CUTS[gi]:starts[c] - GATE_CUTS[gi] + SIZES[c]]
 
+        def cast(t):
+            for h in range(XSPLIT[t]):
+                cols = slice(h * T // XSPLIT[t], (h + 1) * T // XSPLIT[t])
+                copy_on(CAST_ENGINES[t], plane_bf[:, t, cols], plane[t][:, cols])
+
+        def w_copy(i):
+            w_grp[i] = keep.tile([P, WPT, N, 4], BF16, name="w_grp%d" % i, align_bytes=64)
+            if W_ENGINES[i] == "g":
+                copy_on("g", w_grp[i][:], w_raw[i][:].rearrange("p e j n -> p e n j"))
+            else:
+                copy_on(
+                    W_ENGINES[i],
+                    w_grp[i][:].rearrange("p e (c i) j -> p e c j i", i=4),
+                    w_raw[i][:].rearrange("p e j (c i) -> p e c j i", i=4),
+                )
+
+        def w_quant(i):
+            w_codes[i] = keep.tile([P, WPT * N], U32, name="w_codes%d" % i, align_bytes=64)
+            w_scales[i] = keep.tile([P, WPT * N], U8, name="w_scales%d" % i, align_bytes=64)
+            nc.vector.quantize_mx(
+                out=w_codes[i][:].bitcast(FP8X4), scales=w_scales[i][:],
+                in_=w_grp[i][:].rearrange("p e n j -> p (e n j)"),
+            )
+
+        def gather(c, t):
+            n = SIZES[c]
+            if c not in x_grp:
+                if RING > 0 and ROADS[c] == "f":
+                    x_grp[c] = ring.tile([P, n, 4], BF16, name="x_grp%d" % c, tag="x_grp", align_bytes=64)
+                else:
+                    x_grp[c] = keep.tile([P, n, 4], BF16, name="x_grp%d" % c, align_bytes=64)
+            road = ROADS[c] if len(ROADS[c]) == 1 else ROADS[c][t]
+            if road == "b":
+                nc.vector.tensor_copy(x_grp[c][:, :, t], plane[t][:].indirect(some(c)))
+            else:
+                nc.scalar.activation(x_grp[c][:, :, t], plane_bf[:, t, :].indirect(some(c)), COPY)
+
+        def quant(c):
+            n = SIZES[c]
+            if c in SPINS:
+                x_codes[c] = keep.tile([P, n], U32, name="x_codes%d" % c, tag="y%d" % SPINS[c], align_bytes=64)
+            else:
+                x_codes[c] = keep.tile([P, n], U32, name="x_codes%d" % c, align_bytes=64)
+            x_scales[c] = keep.tile([P, n], U8, name="x_scales%d" % c, align_bytes=64)
+            nc.vector.quantize_mx(
+                out=x_codes[c][:].bitcast(FP8X4), scales=x_scales[c][:],
+                in_=x_grp[c][:].rearrange("p n t -> p (n t)"),
+            )
+
+        def mult(c):
+            n = SIZES[c]
+            acc[c] = psum.tile([P, n], F32, name="acc%d" % c)
+            for s in range(n // C):
+                e = starts[c] // C + s
+                here = slice(s * C, (s + 1) * C)
+                wcols = slice((e % WPT) * N, (e % WPT + 1) * N)
+                nc.tensor.matmul_mx(
+                    out=acc[c][:, here],
+                    lhsT=w_codes[e // WPT][:, wcols].bitcast(FP8X4), lhsT_scale=w_scales[e // WPT][:, wcols],
+                    rhs=x_codes[c][:, here].bitcast(FP8X4), rhs_scale=x_scales[c][:, here],
+                    start=True, stop=True,
+                )
+
+        def leave(c):
+            y[c] = keep.tile([P, SIZES[c]], F32, name="y%d" % c, tag="y%d" % c, align_bytes=64)
+            if OUT_ENGINES[c] == "v":
+                nc.vector.tensor_tensor(y[c][:], acc[c][:], gate_of(c), MULT)
+            else:
+                nc.scalar.copy(y[c][:], acc[c][:])
+
         def scatter(c):
             if OUT_ENGINES[c] == "v":
                 nc.vector.tensor_copy(out_w[:].indirect(some(c)), y[c][:])
             else:
                 nc.vector.tensor_tensor(out_w[:].indirect(some(c)), y[c][:], gate_of(c), MULT)
 
-        for c in range(len(SIZES)):
-            n = SIZES[c]
-            if ROADS[c] == "a":
-                x_grp = keep.tile([P, n, 4], BF16, name="x_grp%d" % c, align_bytes=64)
-                g4 = keep.tile([P, 4, n], F32, name="g4_%d" % c)
+        for step in TEXT:
+            kind = step[0]
+            a = int(step[1])
+            if kind == "c":
+                cast(a)
+            elif kind == "W":
+                w_copy(a)
+            elif kind == "Q":
+                w_quant(a)
+            elif kind == "G":
                 for t in range(4):
-                    nc.vector.tensor_copy(g4[:, t, :], plane[t][:].indirect(some(c)))
-                if FAST:
-                    copy_on(
-                        MIX_ENGINE,
-                        x_grp[:].rearrange("p (c i) t -> p c t i", i=4),
-                        g4[:].rearrange("p t (c i) -> p c t i", i=4),
-                    )
-                else:
-                    copy_on(MIX_ENGINE, x_grp[:], g4[:].rearrange("p t n -> p n t"))
-            elif ROADS[c] == "h":
-                x_grp = keep.tile([P, n, 4], BF16, name="x_grp%d" % c, align_bytes=64)
-                for t in range(2):
-                    nc.vector.tensor_copy(x_grp[:, :, t], plane[t][:].indirect(some(c)))
-                for t in range(2, 4):
-                    nc.scalar.activation(x_grp[:, :, t], plane_bf[:, t, :].indirect(some(c)), COPY)
-            elif ROADS[c] == "b":
-                x_grp = keep.tile([P, n, 4], BF16, name="x_grp%d" % c, align_bytes=64)
-                for t in range(4):
-                    nc.vector.tensor_copy(x_grp[:, :, t], plane[t][:].indirect(some(c)))
-            elif ROADS[c] == "f":
-                x_grp = ring.tile([P, n, 4], BF16, name="x_grp%d" % c, tag="x_grp", align_bytes=64)
-                for t in range(4):
-                    nc.scalar.activation(x_grp[:, :, t], plane_bf[:, t, :].indirect(some(c)), COPY)
+                    gather(a, t)
+            elif kind == "g":
+                gather(a, int(step[2]))
+            elif kind == "q":
+                quant(a)
+            elif kind == "m":
+                mult(a)
+            elif kind == "o":
+                leave(a)
             else:
-                x_pair = ring.tile([P, 2, n, 2], BF16, name="x_pair%d" % c, tag="x_pair", align_bytes=64)
-                for t in range(4):
-                    nc.scalar.activation(x_pair[:, t // 2, :, t % 2], plane_bf[:, t, :].indirect(some(c)), COPY)
-                x_grp = keep.tile([P, n, 4], BF16, name="x_grp%d" % c, align_bytes=64)
-                nc.vector.tensor_copy(
-                    x_grp[:].rearrange("p n t -> p (n t)").bitcast(F32).rearrange("p (n u) -> p n u", u=2),
-                    x_pair[:].rearrange("p u n e -> p (u n e)").bitcast(F32).rearrange("p (u n) -> p n u", u=2),
-                )
-            if c in PINS:
-                x_codes = keep.tile([P, n], U32, name="x_codes%d" % c, tag="pin%d" % PINS[c], align_bytes=64)
-            elif c in SPINS:
-                x_codes = keep.tile([P, n], U32, name="x_codes%d" % c, tag="y%d" % SPINS[c], align_bytes=64)
-            else:
-                x_codes = keep.tile([P, n], U32, name="x_codes%d" % c, align_bytes=64)
-            x_scales = keep.tile([P, n], U8, name="x_scales%d" % c, align_bytes=64)
-            nc.vector.quantize_mx(
-                out=x_codes[:].bitcast(FP8X4), scales=x_scales[:],
-                in_=x_grp[:].rearrange("p n t -> p (n t)"),
-            )
-            acc = psum.tile([P, n], F32, name="acc%d" % c)
-            for s in range(n // C):
-                e = starts[c] // C + s
-                here = slice(s * C, (s + 1) * C)
-                wcols = slice((e % 2) * N, (e % 2 + 1) * N)
-                nc.tensor.matmul_mx(
-                    out=acc[:, here],
-                    lhsT=w_codes[e // 2][:, wcols].bitcast(FP8X4), lhsT_scale=w_scales[e // 2][:, wcols],
-                    rhs=x_codes[:, here].bitcast(FP8X4), rhs_scale=x_scales[:, here],
-                    start=True, stop=True,
-                )
-            y.append(keep.tile([P, n], F32, name="y%d" % c, tag="y%d" % c, align_bytes=64))
-            if OUT_ENGINES[c] == "v":
-                nc.vector.tensor_tensor(y[c][:], acc[:], gate_of(c), MULT)
-            else:
-                nc.scalar.copy(y[c][:], acc[:])
-            for d in SCATTER_AFTER[c]:
-                scatter(d)
+                scatter(a)
 
         nc.sync.dma_start(out[:, 0:T], out_w[:, 0:T])

@@ -19,7 +19,8 @@ FLOPS = 2 * K * N * E * C
 SPINS = {}
 SIZES = [256,256,128,128,256]
 ROADS = ["b","f","f","f","f"]
-OUT_ENGINES = ["s","s","s","s","v"]
+OUT_ENGINES = ["s","s","s","s","s"]
+W_BY_EXPERT = [3]
 CAST_ENGINES = ["s","v","v","v"]
 W_ENGINES = ["v","v","v","s"]
 WPT = 2
@@ -96,7 +97,14 @@ def tile_routed_moe_kernel(tc, xT, w, gate, offs, out):
 
         def w_copy(i):
             w_grp[i] = keep.tile([P, WPT, N, 4], BF16, name="w_grp%d" % i, align_bytes=64)
-            if W_ENGINES[i] == "g":
+            if i in W_BY_EXPERT:
+                for e in range(WPT):
+                    copy_on(
+                        W_ENGINES[i],
+                        w_grp[i][:, e].rearrange("p (c i) j -> p c j i", i=4),
+                        w_raw[i][:, e].rearrange("p j (c i) -> p c j i", i=4),
+                    )
+            elif W_ENGINES[i] == "g":
                 copy_on("g", w_grp[i][:], w_raw[i][:].rearrange("p e j n -> p e n j"))
             else:
                 copy_on(
@@ -108,10 +116,17 @@ def tile_routed_moe_kernel(tc, xT, w, gate, offs, out):
         def w_quant(i):
             w_codes[i] = keep.tile([P, WPT * N], U32, name="w_codes%d" % i, align_bytes=64)
             w_scales[i] = keep.tile([P, WPT * N], U8, name="w_scales%d" % i, align_bytes=64)
-            nc.vector.quantize_mx(
-                out=w_codes[i][:].bitcast(FP8X4), scales=w_scales[i][:],
-                in_=w_grp[i][:].rearrange("p e n j -> p (e n j)"),
-            )
+            if i in W_BY_EXPERT:
+                for e in range(WPT):
+                    nc.vector.quantize_mx(
+                        out=w_codes[i][:, e * N:(e + 1) * N].bitcast(FP8X4), scales=w_scales[i][:, e * N:(e + 1) * N],
+                        in_=w_grp[i][:, e].rearrange("p n j -> p (n j)"),
+                    )
+            else:
+                nc.vector.quantize_mx(
+                    out=w_codes[i][:].bitcast(FP8X4), scales=w_scales[i][:],
+                    in_=w_grp[i][:].rearrange("p e n j -> p (e n j)"),
+                )
 
         def gather(c, t):
             n = SIZES[c]

@@ -20,7 +20,7 @@ SPINS = {}
 SIZES = [256,256,128,128,256]
 ROADS = ["b","f","f","f","f"]
 OUT_ENGINES = ["s","s","s","s","s"]
-W_BY_EXPERT = [3]
+W_BY_EXPERT = [0,1,2,3]
 CAST_ENGINES = ["s","v","v","v"]
 W_ENGINES = ["v","v","v","s"]
 WPT = 2

@@ -27,7 +27,7 @@ WPT = 2
 LOAD_ORDER = ["x0","o0","x1","w0","x2","w1","x3","w2","g0","w3","g1"]
 RING = 3
 GATE_CUTS = [0,512,1024]
-XSPLIT = [2,1,1,2]
+XSPLIT = [2,2,2,2]
 TEXT = ["c0","c1","c2","c3","W0","Q0","W1","Q1","W2","Q2","W3","Q3","G0","q0","m0","o0","s0","G1","q1","m1","o1","s1","G2","q2","m2","o2","s2","G3","q3","m3","o3","s3","G4","q4","m4","o4","s4"]
 
 

@@ -20,7 +20,7 @@ SPINS = {}
 SIZES = [256,256,128,128,256]
 ROADS = ["b","f","f","f","f"]
 OUT_ENGINES = ["s","s","s","s","s"]
-W_BY_EXPERT = [0,1,2,3]
+W_BY_EXPERT = [3]
 CAST_ENGINES = ["s","v","v","v"]
 W_ENGINES = ["v","v","v","s"]
 WPT = 2

from contextlib import ExitStack

import concourse.mybir as mybir

F32 = mybir.dt.float32
BF16 = mybir.dt.bfloat16
U32 = mybir.dt.uint32
U16 = mybir.dt.uint16
U8 = mybir.dt.uint8
FP8X4 = mybir.dt.float8_e4m3fn_x4
MULT = mybir.AluOpType.mult
ADD = mybir.AluOpType.add
COPY = mybir.ActivationFunctionType.Copy

P = 128
K, T, E, C, N = 512, 1024, 8, 128, 128
FLOPS = 2 * K * N * E * C

SPINS = {}
SIZES = [256,256,128,128,256]
ROADS = ["b","f","f","f","f"]
OUT_ENGINES = ["s","s","s","s","s"]
W_BY_EXPERT = [3]
CAST_ENGINES = ["s","v","v","v"]
W_ENGINES = ["v","v","v","s"]
WPT = 2
LOAD_ORDER = ["x0","o0","x1","w0","x2","w1","x3","w2","g0","w3","g1"]
RING = 3
GATE_CUTS = [0,512,1024]
XSPLIT = [2,2,2,2]
TEXT = ["c0","c1","c2","c3","W0","Q0","W1","Q1","W2","Q2","W3","Q3","G0","q0","m0","o0","s0","G1","q1","m1","o1","s1","G2","q2","m2","o2","s2","G3","q3","m3","o3","s3","G4","q4","m4","o4","s4"]


def tile_routed_moe_kernel(tc, xT, w, gate, offs, out):
    nc = tc.nc

    def copy_on(engine, dst, src):
        if engine == "v":
            nc.vector.tensor_copy(dst, src)
        elif engine == "s":
            nc.scalar.copy(dst, src)
        else:
            nc.gpsimd.tensor_scalar(dst, src, 1.0, 0.0, MULT, ADD)

    with ExitStack() as ctx:
        lists = ctx.enter_context(tc.tile_pool(name="lists", bufs=1))
        keep = ctx.enter_context(tc.tile_pool(name="keep", bufs=1))
        psum = ctx.enter_context(tc.psum_pool(name="psum", bufs=1))
        ring = ctx.enter_context(tc.tile_pool(name="ring", bufs=max(RING, 1)))

        offs_t = lists.tile([P, E * C // 16], U16, name="offs_t")
        x_view = xT.rearrange("(p t) n -> p t n", t=4)
        plane = [keep.tile([P, T], F32, name="plane%d" % t) for t in range(4)]
        w_raw = [keep.tile([P, WPT, 4, N], F32, name="w_raw%d" % i) for i in range(E // WPT)]
        gate_t = [keep.tile([P, GATE_CUTS[i + 1] - GATE_CUTS[i]], F32, name="gate_t%d" % i) for i in range(len(GATE_CUTS) - 1)]
        for what in LOAD_ORDER:
            i = int(what[1])
            if what[0] == "o":
                nc.sync.dma_start(offs_t[:], offs)
            elif what[0] == "x":
                for h in range(XSPLIT[i]):
                    cols = slice(h * T // XSPLIT[i], (h + 1) * T // XSPLIT[i])
                    nc.sync.dma_start(plane[i][:, cols], x_view[:, i, cols])
            elif what[0] == "w":
                nc.sync.dma_start(w_raw[i][:], w[WPT * i:WPT * i + WPT].rearrange("e (p j) n -> p e j n", j=4))
            else:
                nc.sync.dma_start(gate_t[i][:], gate[:, GATE_CUTS[i]:GATE_CUTS[i + 1]])

        warm_in = keep.tile([P, 1], F32, name="warm_in")
        warm_out = keep.tile([P, 1], F32, name="warm_out")
        nc.vector.memset(warm_in[:], 0.0)
        nc.scalar.activation(warm_out[:], warm_in[:], COPY)

        plane_bf = keep.tile([P, 4, T], BF16, name="plane_bf")
        out_w = keep.tile([P, T], F32, name="out_w")
        starts = [sum(SIZES[:c]) for c in range(len(SIZES))]
        w_grp = {}
        w_codes = {}
        w_scales = {}
        x_grp = {}
        x_codes = {}
        x_scales = {}
        acc = {}
        y = {}

        def some(c):
            return offs_t[:, starts[c] // 16:(starts[c] + SIZES[c]) // 16]

        def gate_of(c):
            gi = max(i for i in range(len(GATE_CUTS) - 1) if GATE_CUTS[i] <= starts[c])
            return gate_t[gi][:, starts[c] - GATE_CUTS[gi]:starts[c] - GATE_CUTS[gi] + SIZES[c]]

        def cast(t):
            for h in range(XSPLIT[t]):
                cols = slice(h * T // XSPLIT[t], (h + 1) * T // XSPLIT[t])
                copy_on(CAST_ENGINES[t], plane_bf[:, t, cols], plane[t][:, cols])

        def w_copy(i):
            w_grp[i] = keep.tile([P, WPT, N, 4], BF16, name="w_grp%d" % i, align_bytes=64)
            if i in W_BY_EXPERT:
                for e in range(WPT):
                    copy_on(
                        W_ENGINES[i],
                        w_grp[i][:, e].rearrange("p (c i) j -> p c j i", i=4),
                        w_raw[i][:, e].rearrange("p j (c i) -> p c j i", i=4),
                    )
            elif W_ENGINES[i] == "g":
                copy_on("g", w_grp[i][:], w_raw[i][:].rearrange("p e j n -> p e n j"))
            else:
                copy_on(
                    W_ENGINES[i],
                    w_grp[i][:].rearrange("p e (c i) j -> p e c j i", i=4),
                    w_raw[i][:].rearrange("p e j (c i) -> p e c j i", i=4),
                )

        def w_quant(i):
            w_codes[i] = keep.tile([P, WPT * N], U32, name="w_codes%d" % i, align_bytes=64)
            w_scales[i] = keep.tile([P, WPT * N], U8, name="w_scales%d" % i, align_bytes=64)
            if i in W_BY_EXPERT:
                for e in range(WPT):
                    nc.vector.quantize_mx(
                        out=w_codes[i][:, e * N:(e + 1) * N].bitcast(FP8X4), scales=w_scales[i][:, e * N:(e + 1) * N],
                        in_=w_grp[i][:, e].rearrange("p n j -> p (n j)"),
                    )
            else:
                nc.vector.quantize_mx(
                    out=w_codes[i][:].bitcast(FP8X4), scales=w_scales[i][:],
                    in_=w_grp[i][:].rearrange("p e n j -> p (e n j)"),
                )

        def gather(c, t):
            n = SIZES[c]
            if c not in x_grp:
                if RING > 0 and ROADS[c] == "f":
                    x_grp[c] = ring.tile([P, n, 4], BF16, name="x_grp%d" % c, tag="x_grp", align_bytes=64)
                else:
                    x_grp[c] = keep.tile([P, n, 4], BF16, name="x_grp%d" % c, align_bytes=64)
            road = ROADS[c] if len(ROADS[c]) == 1 else ROADS[c][t]
            if road == "b":
                nc.vector.tensor_copy(x_grp[c][:, :, t], plane[t][:].indirect(some(c)))
            else:
                nc.scalar.activation(x_grp[c][:, :, t], plane_bf[:, t, :].indirect(some(c)), COPY)

        def quant(c):
            n = SIZES[c]
            if c in SPINS:
                x_codes[c] = keep.tile([P, n], U32, name="x_codes%d" % c, tag="y%d" % SPINS[c], align_bytes=64)
            else:
                x_codes[c] = keep.tile([P, n], U32, name="x_codes%d" % c, align_bytes=64)
            x_scales[c] = keep.tile([P, n], U8, name="x_scales%d" % c, align_bytes=64)
            nc.vector.quantize_mx(
                out=x_codes[c][:].bitcast(FP8X4), scales=x_scales[c][:],
                in_=x_grp[c][:].rearrange("p n t -> p (n t)"),
            )

        def mult(c):
            n = SIZES[c]
            acc[c] = psum.tile([P, n], F32, name="acc%d" % c)
            for s in range(n // C):
                e = starts[c] // C + s
                here = slice(s * C, (s + 1) * C)
                wcols = slice((e % WPT) * N, (e % WPT + 1) * N)
                nc.tensor.matmul_mx(
                    out=acc[c][:, here],
                    lhsT=w_codes[e // WPT][:, wcols].bitcast(FP8X4), lhsT_scale=w_scales[e // WPT][:, wcols],
                    rhs=x_codes[c][:, here].bitcast(FP8X4), rhs_scale=x_scales[c][:, here],
                    start=True, stop=True,
                )

        def leave(c):
            y[c] = keep.tile([P, SIZES[c]], F32, name="y%d" % c, tag="y%d" % c, align_bytes=64)
            if OUT_ENGINES[c] == "v":
                nc.vector.tensor_tensor(y[c][:], acc[c][:], gate_of(c), MULT)
            else:
                nc.scalar.copy(y[c][:], acc[c][:])

        def scatter(c):
            if OUT_ENGINES[c] == "v":
                nc.vector.tensor_copy(out_w[:].indirect(some(c)), y[c][:])
            else:
                nc.vector.tensor_tensor(out_w[:].indirect(some(c)), y[c][:], gate_of(c), MULT)

        for step in TEXT:
            kind = step[0]
            a = int(step[1])
            if kind == "c":
                cast(a)
            elif kind == "W":
                w_copy(a)
            elif kind == "Q":
                w_quant(a)
            elif kind == "G":
                for t in range(4):
                    gather(a, t)
            elif kind == "g":
                gather(a, int(step[2]))
            elif kind == "q":
                quant(a)
            elif kind == "m":
                mult(a)
            elif kind == "o":
                leave(a)
            else:
                scatter(a)

        nc.sync.dma_start(out[:, 0:T], out_w[:, 0:T])
